import numpy as np
import ml_dtypes


def mxq(x, axis, fmt="e4m3"):
    dtype, down = {"e4m3": (ml_dtypes.float8_e4m3fn, 7), "e5m2": (ml_dtypes.float8_e5m2, 14)}[fmt]
    v = np.moveaxis(np.asarray(x, np.float32).astype(ml_dtypes.bfloat16).astype(np.float64), axis, -1)
    blocks = v.reshape(v.shape[:-1] + (-1, 32))
    amax = np.abs(blocks).max(-1, keepdims=True)
    byte = np.maximum(np.where(amax > 0, np.frexp(amax)[1] - 1 + 127, 0) - down, 1)
    scale = np.exp2(byte - 127.0)
    codes = (blocks / scale).astype(np.float32).astype(dtype).astype(np.float64)
    return np.moveaxis((codes * scale).reshape(v.shape), -1, axis)


WIDE = False


def mx_kscale(k):
    if not WIDE:
        return np.ones(k)
    levels = np.array([10, -10, 5, -5, 0])
    if k % 512:
        return np.exp2(np.random.permutation(np.resize(levels, k // 32))).repeat(32)
    a = np.empty((k // 512, 16))
    for p in range(k // 512):
        a[p, :8] = np.random.permutation(np.resize(levels, 8))
        for g in range(8):
            far = levels[np.abs(levels - a[p, g]) >= 10]
            a[p, g + 8] = far[np.random.randint(len(far))]
    return np.exp2(a.ravel()).repeat(32)


def f64(x):
    return np.asarray(x).astype(np.float64)


def striped(idx):
    return np.tile(np.asarray(idx).reshape(-1, 16).T, (8, 1)).astype(np.uint16)


def unstriped(offs):
    return offs[:16].T.reshape(-1).astype(np.int64)


E2M1 = np.array([0.0, 0.5, 1.0, 1.5, 2.0, 3.0, 4.0, 6.0, -0.0, -0.5, -1.0, -1.5, -2.0, -3.0, -4.0, -6.0])


def pack_weight(w, fmt):
    k, n = w.shape
    w = f64(np.asarray(w, np.float32).astype(ml_dtypes.bfloat16)).reshape(k // 32, 32, n)
    amax = np.abs(w).max(1)
    if fmt == "e4m3":
        byte = np.frexp(amax)[1] - 1 + 127 - 7
    else:
        mant, ex = np.frexp(amax / 6.0)
        byte = np.where(mant > 0.5, ex, ex - 1) + 127
    byte = np.clip(np.where(amax > 0, byte, 1), 1, 254)
    scaled = (w * np.exp2(127.0 - byte)[:, None, :]).reshape(k, n).astype(np.float32)
    by_word = np.ascontiguousarray(scaled.reshape(k // 512, 128, 4, n).transpose(0, 1, 3, 2))
    if fmt == "e4m3":
        words = by_word.astype(ml_dtypes.float8_e4m3fn).view(np.uint8)
    else:
        c = by_word.astype(ml_dtypes.float4_e2m1fn).view(np.uint8) & 0xF
        words = (c[..., 0::2] | (c[..., 1::2] << 4)).reshape(k // 512, 128, 2 * n)
    return np.ascontiguousarray(words), np.ascontiguousarray(byte.astype(np.uint8).reshape(k // 512, 16, n))


def unpack_weight(words, scales, fmt):
    g, _, n = scales.shape
    words = np.ascontiguousarray(words).reshape(g, 128, n, -1)
    if fmt == "e4m3":
        vals = words.view(ml_dtypes.float8_e4m3fn).astype(np.float64)
    else:
        nib = np.empty((g, 128, n, 4), np.uint8)
        nib[..., 0::2] = words & 0xF
        nib[..., 1::2] = words >> 4
        vals = E2M1[nib]
    vals = vals * np.repeat(np.exp2(scales.astype(np.float64) - 127.0), 8, axis=1)[..., None]
    return vals.transpose(0, 1, 3, 2).reshape(g * 512, n)


def sigmoid(v):
    return 1.0 / (1.0 + np.exp(-v))


def bf(x):
    return np.asarray(x, np.float32).astype(ml_dtypes.bfloat16)


def planes(Y):
    r, m = Y.shape
    b = f64(bf(Y)).reshape(r // 32, 32, m)
    amax = np.abs(b).max(1)
    byte = np.clip(np.where(amax > 0, np.frexp(amax)[1] - 1 + 127 - 7, 1), 1, 254)
    codes = (b * np.exp2(127.0 - byte)[:, None, :]).reshape(r, m).astype(np.float32).astype(ml_dtypes.float8_e4m3fn).view(np.uint8)
    words = codes.reshape(r // 512, 128, 4, m).transpose(0, 1, 3, 2)
    return np.ascontiguousarray(words), np.ascontiguousarray(byte.astype(np.uint8).reshape(r // 512, 16, m))


D, T, I, Q, E, U, K, M = 512, 2048, 512, 256, 512, 1024, 32, 1024


def setup_inputs():
    n = np.random.standard_normal
    idx = np.random.permutation(T)[:I]
    idx2 = np.random.permutation(U)[:I]
    idx3 = np.random.permutation(M)[:Q]
    fd = mx_kscale(D)
    fi = mx_kscale(I)
    ti = np.ones(T)
    ti[idx] = fi
    keysp = pack_weight(n((D, T)) / fd[:, None], "e2m1")
    return {
        "query": (n((D, Q)) * 1.2 / np.sqrt(D) * fd[:, None]).astype(np.float32),
        "query2": (n((D, Q)) * 1.5 / np.sqrt(D) * fd[:, None]).astype(np.float32),
        "keys_words": keysp[0],
        "keys_scales": keysp[1],
        "notes": (n((D, U)) / fd[:, None]).astype(np.float32),
        "lam": (np.random.uniform(-0.8, 0.8, (Q, 1))).astype(np.float32),
        "sres": (np.random.uniform(1.0, 8.0, (I, 1))).astype(np.float32),
        "os": (np.random.uniform(4.0, 16.0, (1, I)) * fi).astype(np.float32),
        "vals": (n((E, T)) / ti).astype(np.float32),
        "member": (n((E, M))).astype(np.float32),
        "mgain": np.tile(np.random.uniform(0.5, 2.0, M), (128, 1)).astype(np.float32),
        "offs": striped(idx),
        "offs2": striped(idx2),
        "offs3": striped(idx3),
    }


def reference(query, query2, keys_words, keys_scales, notes, lam, sres, os, vals, member, mgain, offs, offs2, offs3):
    idx = unstriped(offs)
    idx2 = unstriped(offs2)
    idx3 = unstriped(offs3)
    keysu = unpack_weight(keys_words, keys_scales, "e2m1")
    queryq = mxq(f64(query), 0, "e4m3")
    keysidxg = keysu[:, idx]
    a = queryq.T @ keysidxg
    query2q = mxq(f64(query2), 0, "e4m3")
    notesidx2q = mxq(f64(notes)[:, idx2], 0, "e4m3")
    b = query2q.T @ notesidx2q
    g1 = sigmoid(b)
    s = a * g1 + (1.0 - g1) * f64(lam)
    p = np.exp(s)
    ptt = p.T
    rg = ptt.reshape(I, K, Q // K).sum(axis=2)
    rv0 = 1.0 / (rg + f64(sres))
    rr = np.repeat(rv0, Q // K, axis=1)
    w0 = ptt * rr
    w = w0.T
    wo1 = w * f64(os)
    wt1 = wo1.T
    vt1 = f64(vals)[:, idx].T
    vt1q = mxq(vt1, 0, "e4m3")
    wt1q = mxq(wt1, 0, "e4m3")
    o = vt1q.T @ wt1q
    y = o * f64(mgain)[:1][:, idx3] + f64(member)[:, idx3]
    words, scales = planes(y)
    return y, words, scales

@@ -1,0 +1,320 @@
+from contextlib import ExitStack
+
+import concourse.mybir as mybir
+from concourse.masks import make_identity
+
+D, T, I, Q, E, U, M = 512, 2048, 512, 256, 512, 1024, 1024
+GROUP = 8
+P = 128
+PACK = 4
+HALVES = Q // P
+KH = P // GROUP
+CHUNK = 512
+
+FLOPS = 2 * D * Q * I * 2 + 2 * I * E * Q
+
+F32 = mybir.dt.float32
+BF16 = mybir.dt.bfloat16
+I32 = mybir.dt.int32
+U32 = mybir.dt.uint32
+U16 = mybir.dt.uint16
+U8 = mybir.dt.uint8
+FP8X4 = mybir.dt.float8_e4m3fn_x4
+FP4X4 = mybir.dt.float4_e2m1fn_x4
+ALU = mybir.AluOpType
+ACT = mybir.ActivationFunctionType
+AX = mybir.AxisListType
+
+
+def tile_attend_tilted_claimants_bymember_pl_kernel(
+    tc, query, query2, keys_words, keys_scales, notes, lam, sres, slot_fac, vals, member, mgain,
+    offs, offs2, offs3, out_0, out_1, out_2,
+):
+    nc = tc.nc
+    with ExitStack() as ctx:
+        sb = ctx.enter_context(tc.tile_pool(name="sb", bufs=1))
+        ps = ctx.enter_context(tc.psum_pool(name="ps", bufs=1))
+
+        def tile(name, shape, dtype, tag=None):
+            return sb.tile(shape, dtype, name=name, tag=tag or name, align_bytes=64)
+
+        def bank(name, tag, shape):
+            return ps.tile(shape, F32, name=name, tag=tag)
+
+        def weave(engine_copy, dst, src):
+            engine_copy(
+                dst.rearrange("p (c i) t -> p c t i", i=PACK),
+                src.rearrange("p t (c i) -> p c t i", i=PACK),
+            )
+
+        def quantize(name, woven, tag=None):
+            width = woven.shape[1]
+            codes = tile(name + "_codes", [P, width], U32, tag)
+            scales = tile(name + "_scales", [P, width], U8)
+            nc.vector.quantize_mx(
+                out=codes[:].bitcast(FP8X4), scales=scales[:], in_=woven.rearrange("p w t -> p (w t)")
+            )
+            return codes, scales
+
+        list_tok = tile("list_tok", [P, I // 16], U16)
+        list_note = tile("list_note", [P, I // 16], U16)
+        list_mem = tile("list_mem", [P, Q // 16], U16)
+        key_words = tile("key_words", [P, T], U16)
+        key_scales = tile("key_scales", [P, T], U8)
+        gain_row = tile("gain_row", [P, M], F32)
+        note_raw = [[tile("note_raw%d%d" % (u, c), [P, 2, CHUNK], F32) for c in range(U // CHUNK)] for u in range(2)]
+        val_pl = [tile("val_pl%d" % t, [P, T], F32) for t in range(PACK)]
+        mem_pl = [tile("mem_pl%d" % t, [P, M], F32) for t in range(PACK)]
+        q1_raw = tile("q1_raw", [P, PACK, Q], F32)
+        q2_raw = tile("q2_raw", [P, PACK, Q], F32)
+        lam_col = tile("lam_col", [P, HALVES], F32)
+        sres_col = tile("sres_col", [P, PACK], F32)
+        os_col = tile("os_col", [P, PACK], F32)
+        ident = tile("ident", [P, P], F32)
+        warm_in = tile("warm_in", [P, 1], F32)
+        warm_out = tile("warm_out", [P, 1], F32)
+
+        notes_v = notes.rearrange("(p t) u -> p t u", t=PACK)
+        vals_v = vals.rearrange("(p t) n -> p t n", t=PACK)
+        member_v = member.rearrange("(p t) m -> p t m", t=PACK)
+        out_v = out_0.rearrange("(p t) q -> p t q", t=PACK)
+
+        def load_notes(u, c):
+            nc.sync.dma_start(note_raw[u][c][:], notes_v[:, 2 * u : 2 * u + 2, c * CHUNK : (c + 1) * CHUNK])
+
+        nc.gpsimd.memset(key_scales[:].bitcast(I32), 0)
+        nc.vector.memset(warm_in[:], 0.0)
+        nc.vector.memset(gain_row[:], 0.0)
+        nc.scalar.activation(warm_out[:], warm_in[:], ACT.Exp)
+        make_identity(nc, ident[:])
+        nc.sync.dma_start(list_tok[:], offs)
+        nc.sync.dma_start(key_words[:].bitcast(I32), keys_words[0].bitcast(I32))
+        load_notes(0, 0)
+        load_notes(0, 1)
+        for quad in range(4):
+            nc.sync.dma_start(
+                key_scales[32 * quad : 32 * quad + 4, :].bitcast(I32),
+                keys_scales[0, 4 * quad : 4 * quad + 4, :].bitcast(I32),
+            )
+        nc.sync.dma_start(list_note[:], offs2)
+        load_notes(1, 0)
+        load_notes(1, 1)
+        nc.sync.dma_start(list_mem[:], offs3)
+        nc.sync.dma_start(gain_row[0:1, :], mgain[0:1, :])
+        nc.sync.dma_start(q1_raw[:], query.rearrange("(p t) q -> p t q", t=PACK))
+        nc.sync.dma_start(q2_raw[:], query2.rearrange("(p t) q -> p t q", t=PACK))
+        with nc.allow_non_contiguous_dma(reason="one value a partition"):
+            nc.sync.dma_start(lam_col[:], lam.rearrange("(h p) o -> p (h o)", p=P))
+        nc.sync.dma_start(val_pl[0][:], vals_v[:, 0, :])
+        nc.sync.dma_start(sres_col[:], sres.rearrange("(p t) o -> p (t o)", t=PACK))
+        nc.sync.dma_start(os_col[:], slot_fac.rearrange("o (p t) -> p (o t)", t=PACK))
+        for t in range(1, PACK):
+            nc.sync.dma_start(val_pl[t][:], vals_v[:, t, :])
+        for t in range(PACK):
+            nc.sync.dma_start(mem_pl[t][:], member_v[:, t, :])
+
+        def pair_up(pairs, raw, c):
+            nc.scalar.copy(
+                pairs[:, c * CHUNK : (c + 1) * CHUNK].bitcast(BF16).rearrange("p (c x) -> p c x", x=2),
+                raw[:].rearrange("p x c -> p c x"),
+            )
+
+        kg_scales = tile("kg_scales", [P, I], U8)
+        kg_words = tile("kg_words", [P, I], U16)
+        note_pairs = [tile("note_pairs%d" % u, [P, U], U32) for u in range(2)]
+        gain_g = tile("gain_g", [P, Q], F32)
+        note_w = tile("note_w", [P, I, PACK], BF16)
+        q1_w = tile("q1_w", [P, Q, PACK], BF16)
+        q2_w = tile("q2_w", [P, Q, PACK], BF16)
+
+        for u in range(2):
+            for c in range(U // CHUNK):
+                pair_up(note_pairs[u], note_raw[u][c], c)
+
+        def gather_notes(u):
+            words = note_w[:].rearrange("p i t -> p (i t)").bitcast(U32).rearrange("p (i u) -> p i u", u=2)
+            nc.vector.tensor_copy(words[:, :, u], note_pairs[u][:].indirect(list_note[:]))
+
+        VCOPY = nc.vector.tensor_copy
+        SCOPY = nc.scalar.copy
+        nc.vector.tensor_copy(kg_words[:], key_words[:].indirect(list_tok[:]))
+        nc.vector.tensor_copy(kg_scales[:], key_scales[:].indirect(list_tok[:]))
+        nc.vector.tensor_copy(gain_g[:], gain_row[:].indirect(list_mem[:]))
+        gather_notes(0)
+        gather_notes(1)
+        weave(SCOPY, q1_w[:], q1_raw[:])
+        weave(SCOPY, q2_w[:], q2_raw[:])
+        q1_codes, q1_scales = quantize("q1", q1_w[:])
+        note_codes, note_scales = quantize("note", note_w[:], "q1_w")
+        q2_codes, q2_scales = quantize("q2", q2_w[:])
+
+        b_ps = [bank("b_ps%d" % h, "b%d" % h, [P, I]) for h in range(HALVES)]
+        a_ps = [bank("a_ps%d" % h, "a%d" % h, [P, I]) for h in range(HALVES)]
+        for h in range(HALVES):
+            rows = slice(h * P, (h + 1) * P)
+            nc.tensor.matmul_mx(
+                out=a_ps[h][:], lhsT=q1_codes[:, rows].bitcast(FP8X4), lhsT_scale=q1_scales[:, rows],
+                rhs=kg_words[:].bitcast(FP4X4), rhs_scale=kg_scales[:], start=True, stop=True,
+            )
+        gaps = [tile("gap%d" % h, [P, I], F32) for h in range(HALVES)]
+        for h in range(HALVES):
+            nc.scalar.activation(gaps[h][:], a_ps[h][:], ACT.Identity, scale=-1.0, bias=lam_col[:, h : h + 1])
+        for h in range(HALVES):
+            rows = slice(h * P, (h + 1) * P)
+            nc.tensor.matmul_mx(
+                out=b_ps[h][:], lhsT=q2_codes[:, rows].bitcast(FP8X4), lhsT_scale=q2_scales[:, rows],
+                rhs=note_codes[:].bitcast(FP8X4), rhs_scale=note_scales[:], start=True, stop=True,
+            )
+
+        val_scales = tile("val_scales", [P, E], U8)
+
+        def quantize_into(codes, scales, cols, woven):
+            nc.vector.quantize_mx(
+                out=codes[:, cols].bitcast(FP8X4), scales=scales[:, cols], in_=woven.rearrange("p w t -> p (w t)")
+            )
+
+        def quantize_values(u, val_codes, val_w):
+            quantize_into(val_codes, val_scales, slice(2 * u * P, (2 * u + 2) * P), val_w[:])
+
+        def gather_values(t):
+            val_g = tile("val_g%d" % t, [P, I], BF16)
+            nc.vector.tensor_copy(val_g[:], val_pl[t][:].indirect(list_tok[:]))
+            return val_g
+
+        def turn_values(t, val_g, val_w):
+            words = val_g[:].bitcast(F32)
+            turned = bank("val_t%d" % t, "v1" if t == 2 else "v0", [P, 2, P])
+            for u in range(2):
+                nc.tensor.transpose(turned[:, u, :], words[:, u : I // 2 : 2], ident[:])
+            part = val_w[:, (t % 2) * P : (t % 2 + 1) * P, :]
+            nc.scalar.copy(
+                part.rearrange("p e t -> p (e t)").bitcast(F32).rearrange("p (e u) -> p e u", u=2),
+                turned[:].rearrange("p u e -> p e u"),
+            )
+
+        p_t = []
+
+        def scores(h):
+            th = tile("th%d" % h, [P, I], F32)
+            nc.scalar.activation(th[:], b_ps[h][:], ACT.Tanh, scale=0.5)
+            gap = gaps[h]
+            mix = tile("mix%d" % h, [P, I], F32, "val_pl0" if h == 0 else None)
+            nc.vector.scalar_tensor_tensor(mix[:], th[:], 1.0, gap[:], ALU.add, ALU.mult)
+            return mix
+
+        def exps(h, mix):
+            p_d = tile("p_d%d" % h, [P, PACK, P], F32)
+            nc.scalar.activation(
+                p_d[:].rearrange("q t s -> q s t"), mix[:].rearrange("q (s t) -> q s t", t=PACK),
+                ACT.Exp, scale=-0.5, bias=lam_col[:, h : h + 1],
+            )
+            turned = bank("p_t%d" % h, "p%d" % h, [P, PACK, P])
+            for t in range(PACK):
+                nc.tensor.transpose(turned[:, t, :], p_d[:, t, :], ident[:])
+            p_t.append(turned)
+
+        den, fac = [
+            [tile("%s%d" % (name, h), [P, KH, PACK], F32) for h in range(HALVES)] for name in ("den", "fac")
+        ]
+
+        def group_sums():
+            total = tile("total", [P, HALVES, KH, PACK], F32, "val_pl1")
+            for h in range(HALVES):
+                nc.vector.tensor_reduce(
+                    total[:, h, :, :], p_t[h][:].rearrange("s t (k j) -> s k t j", j=GROUP), AX.X, ALU.add
+                )
+            for h in range(HALVES):
+                for t in range(PACK):
+                    nc.scalar.activation(den[h][:, :, t], total[:, h, :, t], ACT.Identity, bias=sres_col[:, t : t + 1])
+
+        def factors():
+            rec = tile("rec", [P, HALVES, KH, PACK], F32, "val_pl2")
+            for h in range(HALVES):
+                nc.vector.reciprocal(rec[:, h, :, :], den[h][:])
+            for h in range(HALVES):
+                for t in range(PACK):
+                    nc.scalar.activation(fac[h][:, :, t], rec[:, h, :, t], ACT.Copy, scale=os_col[:, t : t + 1])
+
+        def weights(tag):
+            w_w = tile("w_w", [P, Q, PACK], BF16, tag)
+            for h in range(HALVES):
+                nc.vector.tensor_tensor(
+                    w_w[:, h * P : (h + 1) * P, :].rearrange("s (k j) t -> s k j t", j=GROUP),
+                    p_t[h][:].rearrange("s t (k j) -> s k j t", j=GROUP),
+                    fac[h][:].unsqueeze(2).to_broadcast([P, KH, GROUP, PACK]),
+                    ALU.mult,
+                )
+            return w_w
+
+        val_g0 = gather_values(0)
+        mix0 = scores(0)
+        mix1 = scores(1)
+        exps(0, mix0)
+        exps(1, mix1)
+        gain_t = bank("gain_t", "b0", [P, HALVES, P])
+        for h in range(HALVES):
+            nc.tensor.transpose(gain_t[:, h, :], gain_g[:, h * P : (h + 1) * P], ident[:])
+        gain_col = tile("gain_col", [P, HALVES], F32, "val_pl0")
+        nc.scalar.copy(gain_col[:], gain_t[:, :, 0])
+        val_wa = tile("val_wa", [P, 2 * P, PACK], BF16, "mix1")
+        turn_values(0, val_g0, val_wa)
+        turn_values(1, gather_values(1), val_wa)
+        group_sums()
+        val_wb = tile("val_wb", [P, 2 * P, PACK], BF16)
+        turn_values(2, gather_values(2), val_wb)
+        factors()
+        val_codes = tile("val_codes", [P, E], U32, "den1")
+        quantize_values(0, val_codes, val_wa)
+        turn_values(3, gather_values(3), val_wb)
+        w_codes = tile("w_codes", [P, Q], U32)
+        w_scales = tile("w_scales", [P, Q], U8)
+        y = tile("y", [P, PACK, Q], F32)
+        y_w = [tile("y_w%d" % h, [P, P, PACK], BF16) for h in range(HALVES)]
+        y_codes = tile("y_codes", [P, Q], U32)
+        y_scales = tile("y_scales", [P, Q], U8)
+        back = []
+
+        def product(h, w_w):
+            rows = slice(h * P, (h + 1) * P)
+            quantize_into(w_codes, w_scales, rows, w_w[:, rows, :])
+            o_t = bank("o_t%d" % h, "b%d" % h, [P, E])
+            nc.tensor.matmul_mx(
+                out=o_t[:], lhsT=w_codes[:, rows].bitcast(FP8X4), lhsT_scale=w_scales[:, rows],
+                rhs=val_codes[:].bitcast(FP8X4), rhs_scale=val_scales[:], start=True, stop=True,
+            )
+            gained = tile("gained%d" % h, [P, PACK, P], F32)
+            nc.scalar.activation(
+                gained[:].rearrange("q t e -> q (t e)"), o_t[:], ACT.Copy, scale=gain_col[:, h : h + 1]
+            )
+            back.append(bank("back%d" % h, "a%d" % h, [P, PACK, P]))
+            for t in range(PACK):
+                nc.tensor.transpose(back[h][:, t, :], gained[:, t, :], ident[:])
+
+        def gather_members(tag=None):
+            mem_g = tile("mem_g", [P, PACK, Q], F32, tag)
+            for t in range(PACK):
+                nc.vector.tensor_copy(mem_g[:, t, :], mem_pl[t][:].indirect(list_mem[:]))
+            return mem_g
+
+        def finish(h, mem_g, copy):
+            rows = slice(h * P, (h + 1) * P)
+            nc.vector.tensor_tensor(y[:, :, rows], back[h][:], mem_g[:, :, rows], ALU.add)
+            nc.sync.dma_start(out_v[:, :, rows], y[:, :, rows])
+            weave(copy, y_w[h][:], y[:, :, rows])
+
+        w_w = weights("val_pl3")
+        quantize_values(1, val_codes, val_wb)
+        product(0, w_w)
+        product(1, w_w)
+        mem_g = gather_members("val_pl3")
+        finish(0, mem_g, SCOPY)
+        finish(1, mem_g, VCOPY)
+        for h in range(HALVES):
+            quantize_into(y_codes, y_scales, slice(h * P, (h + 1) * P), y_w[h][:])
+        nc.sync.dma_start(out_1[0].rearrange("p c r -> p (c r)").bitcast(I32), y_codes[:].bitcast(I32))
+        for quad in range(4):
+            queue = nc.scalar if quad % 2 else nc.sync
+            queue.dma_start(
+                out_2[0, 4 * quad : 4 * quad + 4, :].bitcast(I32),
+                y_scales[32 * quad : 32 * quad + 4, :].bitcast(I32),
+            )

@@ -56,6 +56,11 @@ def tile_attend_tilted_claimants_bymember_pl_kernel(
             )
             return codes, scales
 
+        def quantize_into(codes, scales, cols, woven):
+            nc.vector.quantize_mx(
+                out=codes[:, cols].bitcast(FP8X4), scales=scales[:, cols], in_=woven.rearrange("p w t -> p (w t)")
+            )
+
         list_tok = tile("list_tok", [P, I // 16], U16)
         list_note = tile("list_note", [P, I // 16], U16)
         list_mem = tile("list_mem", [P, Q // 16], U16)
@@ -84,6 +89,8 @@ def tile_attend_tilted_claimants_bymember_pl_kernel(
 
         nc.gpsimd.memset(key_scales[:].bitcast(I32), 0)
         nc.vector.memset(warm_in[:], 0.0)
+        lam_rows = tile("lam_rows", [P, P], F32)
+        nc.vector.memset(lam_rows[:], 0.0)
         nc.vector.memset(gain_row[:], 0.0)
         nc.scalar.activation(warm_out[:], warm_in[:], ACT.Exp)
         make_identity(nc, ident[:])
@@ -91,27 +98,26 @@ def tile_attend_tilted_claimants_bymember_pl_kernel(
         nc.sync.dma_start(key_words[:].bitcast(I32), keys_words[0].bitcast(I32))
         load_notes(0, 0)
         load_notes(0, 1)
-        for quad in range(4):
-            nc.sync.dma_start(
-                key_scales[32 * quad : 32 * quad + 4, :].bitcast(I32),
-                keys_scales[0, 4 * quad : 4 * quad + 4, :].bitcast(I32),
-            )
+        for row in range(4):
+            nc.sync.dma_start(key_scales[row:P:32, :].bitcast(I32), keys_scales[0, row:16:4, :].bitcast(I32))
         nc.sync.dma_start(list_note[:], offs2)
         load_notes(1, 0)
         load_notes(1, 1)
-        nc.sync.dma_start(list_mem[:], offs3)
-        nc.sync.dma_start(gain_row[0:1, :], mgain[0:1, :])
+        nc.sync.dma_start(lam_rows[0:HALVES, :], lam.rearrange("(h p) o -> h (p o)", p=P))
         nc.sync.dma_start(q1_raw[:], query.rearrange("(p t) q -> p t q", t=PACK))
         nc.sync.dma_start(q2_raw[:], query2.rearrange("(p t) q -> p t q", t=PACK))
-        with nc.allow_non_contiguous_dma(reason="one value a partition"):
-            nc.sync.dma_start(lam_col[:], lam.rearrange("(h p) o -> p (h o)", p=P))
         nc.sync.dma_start(val_pl[0][:], vals_v[:, 0, :])
+        nc.sync.dma_start(val_pl[1][:], vals_v[:, 1, :])
+        nc.sync.dma_start(list_mem[:], offs3)
+        nc.sync.dma_start(gain_row[0:1, :], mgain[0:1, :])
         nc.sync.dma_start(sres_col[:], sres.rearrange("(p t) o -> p (t o)", t=PACK))
+        nc.sync.dma_start(val_pl[2][:], vals_v[:, 2, :])
         nc.sync.dma_start(os_col[:], slot_fac.rearrange("o (p t) -> p (o t)", t=PACK))
-        for t in range(1, PACK):
-            nc.sync.dma_start(val_pl[t][:], vals_v[:, t, :])
-        for t in range(PACK):
-            nc.sync.dma_start(mem_pl[t][:], member_v[:, t, :])
+        nc.sync.dma_start(val_pl[3][:], vals_v[:, 3, :])
+        nc.sync.dma_start(mem_pl[0][:], member_v[:, 0, :])
+        nc.sync.dma_start(mem_pl[1][:], member_v[:, 1, :])
+        nc.sync.dma_start(mem_pl[2][:], member_v[:, 2, :])
+        nc.sync.dma_start(mem_pl[3][:], member_v[:, 3, :])
 
         def pair_up(pairs, raw, c):
             nc.scalar.copy(
@@ -137,16 +143,27 @@ def tile_attend_tilted_claimants_bymember_pl_kernel(
 
         VCOPY = nc.vector.tensor_copy
         SCOPY = nc.scalar.copy
+        q1_codes, q2_codes = [tile(name, [P, Q], U32) for name in ("q1_codes", "q2_codes")]
+        q1_scales, q2_scales = [tile(name, [P, Q], U8) for name in ("q1_scales", "q2_scales")]
+
+        def query_half(raw, woven, codes, scales, h):
+            rows = slice(h * P, (h + 1) * P)
+            weave(SCOPY, woven[:, rows, :], raw[:, :, rows])
+            quantize_into(codes, scales, rows, woven[:, rows, :])
+
         nc.vector.tensor_copy(kg_words[:], key_words[:].indirect(list_tok[:]))
         nc.vector.tensor_copy(kg_scales[:], key_scales[:].indirect(list_tok[:]))
-        nc.vector.tensor_copy(gain_g[:], gain_row[:].indirect(list_mem[:]))
         gather_notes(0)
         gather_notes(1)
-        weave(SCOPY, q1_w[:], q1_raw[:])
-        weave(SCOPY, q2_w[:], q2_raw[:])
-        q1_codes, q1_scales = quantize("q1", q1_w[:])
-        note_codes, note_scales = quantize("note", note_w[:], "q1_w")
-        q2_codes, q2_scales = quantize("q2", q2_w[:])
+        query_half(q1_raw, q1_w, q1_codes, q1_scales, 0)
+        query_half(q1_raw, q1_w, q1_codes, q1_scales, 1)
+        note_codes, note_scales = quantize("note", note_w[:], "q1_raw")
+        query_half(q2_raw, q2_w, q2_codes, q2_scales, 0)
+        query_half(q2_raw, q2_w, q2_codes, q2_scales, 1)
+
+        lam_t = bank("lam_t", "v1", [P, P])
+        nc.tensor.transpose(lam_t[:], lam_rows[:], ident[:])
+        nc.vector.tensor_copy(lam_col[:], lam_t[:, 0:HALVES])
 
         b_ps = [bank("b_ps%d" % h, "b%d" % h, [P, I]) for h in range(HALVES)]
         a_ps = [bank("a_ps%d" % h, "a%d" % h, [P, I]) for h in range(HALVES)]
@@ -167,11 +184,6 @@ def tile_attend_tilted_claimants_bymember_pl_kernel(
             )
 
         val_scales = tile("val_scales", [P, E], U8)
-
-        def quantize_into(codes, scales, cols, woven):
-            nc.vector.quantize_mx(
-                out=codes[:, cols].bitcast(FP8X4), scales=scales[:, cols], in_=woven.rearrange("p w t -> p (w t)")
-            )
 
         def quantize_values(u, val_codes, val_w):
             quantize_into(val_codes, val_scales, slice(2 * u * P, (2 * u + 2) * P), val_w[:])
@@ -251,19 +263,15 @@ def tile_attend_tilted_claimants_bymember_pl_kernel(
         mix1 = scores(1)
         exps(0, mix0)
         exps(1, mix1)
-        gain_t = bank("gain_t", "b0", [P, HALVES, P])
-        for h in range(HALVES):
-            nc.tensor.transpose(gain_t[:, h, :], gain_g[:, h * P : (h + 1) * P], ident[:])
-        gain_col = tile("gain_col", [P, HALVES], F32, "val_pl0")
-        nc.scalar.copy(gain_col[:], gain_t[:, :, 0])
         val_wa = tile("val_wa", [P, 2 * P, PACK], BF16, "mix1")
         turn_values(0, val_g0, val_wa)
         turn_values(1, gather_values(1), val_wa)
+        nc.vector.tensor_copy(gain_g[:], gain_row[:].indirect(list_mem[:]))
         group_sums()
         val_wb = tile("val_wb", [P, 2 * P, PACK], BF16)
         turn_values(2, gather_values(2), val_wb)
         factors()
-        val_codes = tile("val_codes", [P, E], U32, "den1")
+        val_codes = tile("val_codes", [P, E], U32, "den0")
         quantize_values(0, val_codes, val_wa)
         turn_values(3, gather_values(3), val_wb)
         w_codes = tile("w_codes", [P, Q], U32)
@@ -274,9 +282,8 @@ def tile_attend_tilted_claimants_bymember_pl_kernel(
         y_scales = tile("y_scales", [P, Q], U8)
         back = []
 
-        def product(h, w_w):
+        def product(h):
             rows = slice(h * P, (h + 1) * P)
-            quantize_into(w_codes, w_scales, rows, w_w[:, rows, :])
             o_t = bank("o_t%d" % h, "b%d" % h, [P, E])
             nc.tensor.matmul_mx(
                 out=o_t[:], lhsT=w_codes[:, rows].bitcast(FP8X4), lhsT_scale=w_scales[:, rows],
@@ -303,10 +310,17 @@ def tile_attend_tilted_claimants_bymember_pl_kernel(
             weave(copy, y_w[h][:], y[:, :, rows])
 
         w_w = weights("val_pl3")
+        for h in range(HALVES):
+            quantize_into(w_codes, w_scales, slice(h * P, (h + 1) * P), w_w[:, h * P : (h + 1) * P, :])
         quantize_values(1, val_codes, val_wb)
-        product(0, w_w)
-        product(1, w_w)
-        mem_g = gather_members("val_pl3")
+        gain_t = bank("gain_t", "p0", [P, HALVES, P])
+        for h in range(HALVES):
+            nc.tensor.transpose(gain_t[:, h, :], gain_g[:, h * P : (h + 1) * P], ident[:])
+        gain_col = tile("gain_col", [P, HALVES], F32)
+        nc.scalar.copy(gain_col[:], gain_t[:, :, 0])
+        product(0)
+        product(1)
+        mem_g = gather_members("fac1")
         finish(0, mem_g, SCOPY)
         finish(1, mem_g, VCOPY)
         for h in range(HALVES):

@@ -4,12 +4,14 @@ import concourse.mybir as mybir
 from concourse.masks import make_identity
 
 D, T, I, Q, E, U, M = 512, 2048, 512, 256, 512, 1024, 1024
-GROUP = 8
 P = 128
 PACK = 4
+GROUP = 8
 HALVES = Q // P
-KH = P // GROUP
-CHUNK = 512
+GROUPS = P // GROUP
+PER_COLUMN = 16
+QUADRANT = 32
+SCALE_ROWS = 16
 
 FLOPS = 2 * D * Q * I * 2 + 2 * I * E * Q
 
@@ -26,8 +28,12 @@ ACT = mybir.ActivationFunctionType
 AX = mybir.AxisListType
 
 
+def run_of(index, width):
+    return slice(index * width, (index + 1) * width)
+
+
 def tile_attend_tilted_claimants_bymember_pl_kernel(
-    tc, query, query2, keys_words, keys_scales, notes, lam, sres, slot_fac, vals, member, mgain,
+    tc, query, query2, keys_words, keys_scales, notes, lam, sres, slot_factor, vals, member, mgain,
     offs, offs2, offs3, out_0, out_1, out_2,
 ):
     nc = tc.nc
@@ -41,294 +47,271 @@ def tile_attend_tilted_claimants_bymember_pl_kernel(
         def bank(name, tag, shape):
             return ps.tile(shape, F32, name=name, tag=tag)
 
-        def weave(engine_copy, dst, src):
-            engine_copy(
-                dst.rearrange("p (c i) t -> p c t i", i=PACK),
-                src.rearrange("p t (c i) -> p c t i", i=PACK),
+        def weave(copy, woven, planes):
+            copy(
+                woven.rearrange("p (c i) t -> p c t i", i=PACK),
+                planes.rearrange("p t (c i) -> p c t i", i=PACK),
             )
 
-        def quantize(name, woven, tag=None):
-            width = woven.shape[1]
-            codes = tile(name + "_codes", [P, width], U32, tag)
-            scales = tile(name + "_scales", [P, width], U8)
-            nc.vector.quantize_mx(
-                out=codes[:].bitcast(FP8X4), scales=scales[:], in_=woven.rearrange("p w t -> p (w t)")
-            )
-            return codes, scales
-
-        def quantize_into(codes, scales, cols, woven):
+        def quantize(codes, scales, cols, woven):
             nc.vector.quantize_mx(
                 out=codes[:, cols].bitcast(FP8X4), scales=scales[:, cols], in_=woven.rearrange("p w t -> p (w t)")
             )
 
-        list_tok = tile("list_tok", [P, I // 16], U16)
-        list_note = tile("list_note", [P, I // 16], U16)
-        list_mem = tile("list_mem", [P, Q // 16], U16)
+        def gather(out, window, entries):
+            nc.vector.tensor_copy(out, window.indirect(entries))
+
+        token_list = tile("token_list", [P, I // PER_COLUMN], U16)
+        note_list = tile("note_list", [P, I // PER_COLUMN], U16)
+        member_list = tile("member_list", [P, Q // PER_COLUMN], U16)
         key_words = tile("key_words", [P, T], U16)
         key_scales = tile("key_scales", [P, T], U8)
         gain_row = tile("gain_row", [P, M], F32)
-        note_raw = [[tile("note_raw%d%d" % (u, c), [P, 2, CHUNK], F32) for c in range(U // CHUNK)] for u in range(2)]
-        val_pl = [tile("val_pl%d" % t, [P, T], F32) for t in range(PACK)]
-        mem_pl = [tile("mem_pl%d" % t, [P, M], F32) for t in range(PACK)]
-        q1_raw = tile("q1_raw", [P, PACK, Q], F32)
-        q2_raw = tile("q2_raw", [P, PACK, Q], F32)
+        note_planes = [tile("note_planes%d" % u, [P, 2, U], F32) for u in range(2)]
+        value_plane = {t: tile("value_plane%d" % t, [P, T], F32) for t in (0, 1, 3)}
+        value2_part = [tile("value2_part%d" % c, [P, T // 2], F32) for c in range(2)]
+        member_plane = [tile("member_plane%d" % t, [P, M], F32) for t in range(PACK)]
+        q1_planes = tile("q1_planes", [P, PACK, Q], F32)
+        q2_planes = tile("q2_planes", [P, PACK, Q], F32)
         lam_col = tile("lam_col", [P, HALVES], F32)
         sres_col = tile("sres_col", [P, PACK], F32)
         os_col = tile("os_col", [P, PACK], F32)
         ident = tile("ident", [P, P], F32)
-        warm_in = tile("warm_in", [P, 1], F32)
-        warm_out = tile("warm_out", [P, 1], F32)
+        lam_rows = tile("lam_rows", [P, P], F32)
 
         notes_v = notes.rearrange("(p t) u -> p t u", t=PACK)
         vals_v = vals.rearrange("(p t) n -> p t n", t=PACK)
         member_v = member.rearrange("(p t) m -> p t m", t=PACK)
         out_v = out_0.rearrange("(p t) q -> p t q", t=PACK)
 
-        def load_notes(u, c):
-            nc.sync.dma_start(note_raw[u][c][:], notes_v[:, 2 * u : 2 * u + 2, c * CHUNK : (c + 1) * CHUNK])
-
         nc.gpsimd.memset(key_scales[:].bitcast(I32), 0)
-        nc.vector.memset(warm_in[:], 0.0)
-        lam_rows = tile("lam_rows", [P, P], F32)
         nc.vector.memset(lam_rows[:], 0.0)
         nc.vector.memset(gain_row[:], 0.0)
-        nc.scalar.activation(warm_out[:], warm_in[:], ACT.Exp)
         make_identity(nc, ident[:])
-        nc.sync.dma_start(list_tok[:], offs)
+
+        nc.sync.dma_start(token_list[:], offs)
         nc.sync.dma_start(key_words[:].bitcast(I32), keys_words[0].bitcast(I32))
-        load_notes(0, 0)
-        load_notes(0, 1)
-        for row in range(4):
-            nc.sync.dma_start(key_scales[row:P:32, :].bitcast(I32), keys_scales[0, row:16:4, :].bitcast(I32))
-        nc.sync.dma_start(list_note[:], offs2)
-        load_notes(1, 0)
-        load_notes(1, 1)
+        nc.sync.dma_start(note_planes[0][:], notes_v[:, 0:2, :])
+        for r in range(PACK):
+            nc.sync.dma_start(
+                key_scales[r:P:QUADRANT, :].bitcast(I32), keys_scales[0, r:SCALE_ROWS:PACK, :].bitcast(I32)
+            )
+        nc.sync.dma_start(note_list[:], offs2)
+        nc.sync.dma_start(note_planes[1][:], notes_v[:, 2:4, :])
         nc.sync.dma_start(lam_rows[0:HALVES, :], lam.rearrange("(h p) o -> h (p o)", p=P))
-        nc.sync.dma_start(q1_raw[:], query.rearrange("(p t) q -> p t q", t=PACK))
-        nc.sync.dma_start(q2_raw[:], query2.rearrange("(p t) q -> p t q", t=PACK))
-        nc.sync.dma_start(val_pl[0][:], vals_v[:, 0, :])
-        nc.sync.dma_start(val_pl[1][:], vals_v[:, 1, :])
-        nc.sync.dma_start(list_mem[:], offs3)
+        nc.sync.dma_start(q1_planes[:], query.rearrange("(p t) q -> p t q", t=PACK))
+        nc.sync.dma_start(q2_planes[:], query2.rearrange("(p t) q -> p t q", t=PACK))
+        for t in range(2):
+            nc.sync.dma_start(value_plane[t][:], vals_v[:, t, :])
+        nc.sync.dma_start(member_list[:], offs3)
         nc.sync.dma_start(gain_row[0:1, :], mgain[0:1, :])
         nc.sync.dma_start(sres_col[:], sres.rearrange("(p t) o -> p (t o)", t=PACK))
-        nc.sync.dma_start(val_pl[2][:], vals_v[:, 2, :])
-        nc.sync.dma_start(os_col[:], slot_fac.rearrange("o (p t) -> p (o t)", t=PACK))
-        nc.sync.dma_start(val_pl[3][:], vals_v[:, 3, :])
-        nc.sync.dma_start(mem_pl[0][:], member_v[:, 0, :])
-        nc.sync.dma_start(mem_pl[1][:], member_v[:, 1, :])
-        nc.sync.dma_start(mem_pl[2][:], member_v[:, 2, :])
-        nc.sync.dma_start(mem_pl[3][:], member_v[:, 3, :])
+        for c in range(2):
+            nc.sync.dma_start(value2_part[c][:], vals_v[:, 2, run_of(c, T // 2)])
+        nc.sync.dma_start(os_col[:], slot_factor.rearrange("o (p t) -> p (o t)", t=PACK))
+        nc.sync.dma_start(value_plane[3][:], vals_v[:, 3, :])
+        for t in range(PACK):
+            nc.sync.dma_start(member_plane[t][:], member_v[:, t, :])
 
-        def pair_up(pairs, raw, c):
-            nc.scalar.copy(
-                pairs[:, c * CHUNK : (c + 1) * CHUNK].bitcast(BF16).rearrange("p (c x) -> p c x", x=2),
-                raw[:].rearrange("p x c -> p c x"),
-            )
-
-        kg_scales = tile("kg_scales", [P, I], U8)
-        kg_words = tile("kg_words", [P, I], U16)
+        picked_key_scales = tile("picked_key_scales", [P, I], U8)
+        picked_key_words = tile("picked_key_words", [P, I], U16)
         note_pairs = [tile("note_pairs%d" % u, [P, U], U32) for u in range(2)]
-        gain_g = tile("gain_g", [P, Q], F32)
-        note_w = tile("note_w", [P, I, PACK], BF16)
-        q1_w = tile("q1_w", [P, Q, PACK], BF16)
-        q2_w = tile("q2_w", [P, Q, PACK], BF16)
-
-        for u in range(2):
-            for c in range(U // CHUNK):
-                pair_up(note_pairs[u], note_raw[u][c], c)
-
-        def gather_notes(u):
-            words = note_w[:].rearrange("p i t -> p (i t)").bitcast(U32).rearrange("p (i u) -> p i u", u=2)
-            nc.vector.tensor_copy(words[:, :, u], note_pairs[u][:].indirect(list_note[:]))
-
-        VCOPY = nc.vector.tensor_copy
-        SCOPY = nc.scalar.copy
+        picked_gain = tile("picked_gain", [P, Q], F32)
+        note_woven = tile("note_woven", [P, I, PACK], BF16)
+        q1_woven = tile("q1_woven", [P, Q, PACK], BF16)
+        q2_woven = tile("q2_woven", [P, Q, PACK], BF16)
         q1_codes, q2_codes = [tile(name, [P, Q], U32) for name in ("q1_codes", "q2_codes")]
         q1_scales, q2_scales = [tile(name, [P, Q], U8) for name in ("q1_scales", "q2_scales")]
 
-        def query_half(raw, woven, codes, scales, h):
-            rows = slice(h * P, (h + 1) * P)
-            weave(SCOPY, woven[:, rows, :], raw[:, :, rows])
-            quantize_into(codes, scales, rows, woven[:, rows, :])
+        def scalar_cast(out, in_):
+            nc.scalar.activation(out, in_, ACT.Copy)
 
-        nc.vector.tensor_copy(kg_words[:], key_words[:].indirect(list_tok[:]))
-        nc.vector.tensor_copy(kg_scales[:], key_scales[:].indirect(list_tok[:]))
-        gather_notes(0)
-        gather_notes(1)
-        query_half(q1_raw, q1_w, q1_codes, q1_scales, 0)
-        query_half(q1_raw, q1_w, q1_codes, q1_scales, 1)
-        note_codes, note_scales = quantize("note", note_w[:], "q1_raw")
-        query_half(q2_raw, q2_w, q2_codes, q2_scales, 0)
-        query_half(q2_raw, q2_w, q2_codes, q2_scales, 1)
+        def pick_notes(u):
+            for c, copy in enumerate((scalar_cast, nc.vector.tensor_copy)):
+                cols = run_of(c, U // 2)
+                copy(
+                    note_pairs[u][:, cols].bitcast(BF16).rearrange("p (c x) -> p c x", x=2),
+                    note_planes[u][:, :, cols].rearrange("p x c -> p c x"),
+                )
+            halves = note_woven[:].rearrange("p i t -> p (i t)").bitcast(U32).rearrange("p (i u) -> p i u", u=2)
+            gather(halves[:, :, u], note_pairs[u][:], note_list[:])
 
-        lam_t = bank("lam_t", "v1", [P, P])
-        nc.tensor.transpose(lam_t[:], lam_rows[:], ident[:])
-        nc.vector.tensor_copy(lam_col[:], lam_t[:, 0:HALVES])
+        def quantize_queries(planes, woven, codes, scales):
+            for h in range(HALVES):
+                rows = run_of(h, P)
+                weave(nc.scalar.copy, woven[:, rows, :], planes[:, :, rows])
+                quantize(codes, scales, rows, woven[:, rows, :])
 
-        b_ps = [bank("b_ps%d" % h, "b%d" % h, [P, I]) for h in range(HALVES)]
-        a_ps = [bank("a_ps%d" % h, "a%d" % h, [P, I]) for h in range(HALVES)]
+        gather(picked_key_words[:], key_words[:], token_list[:])
+        gather(picked_key_scales[:], key_scales[:], token_list[:])
+        for u in range(2):
+            pick_notes(u)
+        quantize_queries(q1_planes, q1_woven, q1_codes, q1_scales)
+        note_codes = tile("note_codes", [P, I], U32, "q1_planes")
+        note_scales = tile("note_scales", [P, I], U8)
+        quantize(note_codes, note_scales, run_of(0, I), note_woven[:])
+        quantize_queries(q2_planes, q2_woven, q2_codes, q2_scales)
+
+        lam_turned = bank("lam_turned", "v1", [P, P])
+        nc.tensor.transpose(lam_turned[:], lam_rows[:], ident[:])
+        nc.vector.tensor_copy(lam_col[:], lam_turned[:, 0:HALVES])
+
+        b_sum = [bank("b_sum%d" % h, "b%d" % h, [P, I]) for h in range(HALVES)]
+        a_sum = [bank("a_sum%d" % h, "a%d" % h, [P, I]) for h in range(HALVES)]
         for h in range(HALVES):
-            rows = slice(h * P, (h + 1) * P)
+            rows = run_of(h, P)
             nc.tensor.matmul_mx(
-                out=a_ps[h][:], lhsT=q1_codes[:, rows].bitcast(FP8X4), lhsT_scale=q1_scales[:, rows],
-                rhs=kg_words[:].bitcast(FP4X4), rhs_scale=kg_scales[:], start=True, stop=True,
+                out=a_sum[h][:], lhsT=q1_codes[:, rows].bitcast(FP8X4), lhsT_scale=q1_scales[:, rows],
+                rhs=picked_key_words[:].bitcast(FP4X4), rhs_scale=picked_key_scales[:], start=True, stop=True,
             )
-        gaps = [tile("gap%d" % h, [P, I], F32) for h in range(HALVES)]
+        gap = [tile("gap%d" % h, [P, I], F32) for h in range(HALVES)]
         for h in range(HALVES):
-            nc.scalar.activation(gaps[h][:], a_ps[h][:], ACT.Identity, scale=-1.0, bias=lam_col[:, h : h + 1])
+            nc.scalar.activation(gap[h][:], a_sum[h][:], ACT.Identity, scale=-1.0, bias=lam_col[:, h : h + 1])
         for h in range(HALVES):
-            rows = slice(h * P, (h + 1) * P)
+            rows = run_of(h, P)
             nc.tensor.matmul_mx(
-                out=b_ps[h][:], lhsT=q2_codes[:, rows].bitcast(FP8X4), lhsT_scale=q2_scales[:, rows],
+                out=b_sum[h][:], lhsT=q2_codes[:, rows].bitcast(FP8X4), lhsT_scale=q2_scales[:, rows],
                 rhs=note_codes[:].bitcast(FP8X4), rhs_scale=note_scales[:], start=True, stop=True,
             )
 
-        val_scales = tile("val_scales", [P, E], U8)
+        value_scales = tile("value_scales", [P, E], U8)
 
-        def quantize_values(u, val_codes, val_w):
-            quantize_into(val_codes, val_scales, slice(2 * u * P, (2 * u + 2) * P), val_w[:])
+        def pick_values(t):
+            picked = tile("picked_values%d" % t, [P, I], BF16)
+            gather(picked[:], value_plane[t][:], token_list[:])
+            return picked
 
-        def gather_values(t):
-            val_g = tile("val_g%d" % t, [P, I], BF16)
-            nc.vector.tensor_copy(val_g[:], val_pl[t][:].indirect(list_tok[:]))
-            return val_g
-
-        def turn_values(t, val_g, val_w):
-            words = val_g[:].bitcast(F32)
-            turned = bank("val_t%d" % t, "v1" if t == 2 else "v0", [P, 2, P])
+        def turn_values(name, tag, picked, woven):
+            pairs = picked[:].bitcast(F32)
+            turned = bank(name, tag, [P, 2, P])
             for u in range(2):
-                nc.tensor.transpose(turned[:, u, :], words[:, u : I // 2 : 2], ident[:])
-            part = val_w[:, (t % 2) * P : (t % 2 + 1) * P, :]
+                nc.tensor.transpose(turned[:, u, :], pairs[:, u : I // 2 : 2], ident[:])
             nc.scalar.copy(
-                part.rearrange("p e t -> p (e t)").bitcast(F32).rearrange("p (e u) -> p e u", u=2),
-                turned[:].rearrange("p u e -> p e u"),
+                woven.rearrange("s e t -> s (e t)").bitcast(F32).rearrange("s (e u) -> s e u", u=2),
+                turned[:].rearrange("s u e -> s e u"),
             )
 
-        p_t = []
-
-        def scores(h):
-            th = tile("th%d" % h, [P, I], F32)
-            nc.scalar.activation(th[:], b_ps[h][:], ACT.Tanh, scale=0.5)
-            gap = gaps[h]
-            mix = tile("mix%d" % h, [P, I], F32, "val_pl0" if h == 0 else None)
-            nc.vector.scalar_tensor_tensor(mix[:], th[:], 1.0, gap[:], ALU.add, ALU.mult)
-            return mix
-
-        def exps(h, mix):
-            p_d = tile("p_d%d" % h, [P, PACK, P], F32)
+        picked0 = pick_values(0)
+        gated = []
+        for h, tag in enumerate(("value_plane0", None)):
+            tanh_b = tile("tanh_b%d" % h, [P, I], F32)
+            nc.scalar.activation(tanh_b[:], b_sum[h][:], ACT.Tanh, scale=0.5)
+            gated.append(tile("gated%d" % h, [P, I], F32, tag))
+            nc.vector.scalar_tensor_tensor(gated[h][:], tanh_b[:], 1.0, gap[h][:], ALU.add, ALU.mult)
+        p_turned = []
+        for h in range(HALVES):
+            p_dealt = tile("p_dealt%d" % h, [P, PACK, P], F32)
             nc.scalar.activation(
-                p_d[:].rearrange("q t s -> q s t"), mix[:].rearrange("q (s t) -> q s t", t=PACK),
+                p_dealt[:].rearrange("q t s -> q s t"), gated[h][:].rearrange("q (s t) -> q s t", t=PACK),
                 ACT.Exp, scale=-0.5, bias=lam_col[:, h : h + 1],
             )
-            turned = bank("p_t%d" % h, "p%d" % h, [P, PACK, P])
+            p_turned.append(bank("p_turned%d" % h, "p%d" % h, [P, PACK, P]))
             for t in range(PACK):
-                nc.tensor.transpose(turned[:, t, :], p_d[:, t, :], ident[:])
-            p_t.append(turned)
+                nc.tensor.transpose(p_turned[h][:, t, :], p_dealt[:, t, :], ident[:])
 
-        den, fac = [
-            [tile("%s%d" % (name, h), [P, KH, PACK], F32) for h in range(HALVES)] for name in ("den", "fac")
-        ]
+        woven0 = tile("value_woven0", [P, P, PACK], BF16, "gated1")
+        turn_values("value_turned0", "v0", picked0, woven0[:])
+        picked1 = pick_values(1)
+        gather(picked_gain[:], gain_row[:], member_list[:])
 
-        def group_sums():
-            total = tile("total", [P, HALVES, KH, PACK], F32, "val_pl1")
-            for h in range(HALVES):
-                nc.vector.tensor_reduce(
-                    total[:, h, :, :], p_t[h][:].rearrange("s t (k j) -> s k t j", j=GROUP), AX.X, ALU.add
-                )
-            for h in range(HALVES):
-                for t in range(PACK):
-                    nc.scalar.activation(den[h][:, :, t], total[:, h, :, t], ACT.Identity, bias=sres_col[:, t : t + 1])
+        denom = [tile("denom%d" % h, [P, GROUPS, PACK], F32) for h in range(HALVES)]
+        inverse = [tile("inverse%d" % h, [P, GROUPS, PACK], F32) for h in range(HALVES)]
+        total = tile("total", [P, HALVES, GROUPS, PACK], F32, "value_plane1")
+        for h in range(HALVES):
+            nc.vector.tensor_reduce(
+                total[:, h, :, :], p_turned[h][:].rearrange("s t (k j) -> s k t j", j=GROUP), AX.X, ALU.add
+            )
+        for h in range(HALVES):
+            nc.vector.tensor_tensor(
+                denom[h][:], total[:, h, :, :], sres_col[:].unsqueeze(1).to_broadcast([P, GROUPS, PACK]), ALU.add
+            )
+        for h in range(HALVES):
+            nc.vector.reciprocal(inverse[h][:], denom[h][:])
 
-        def factors():
-            rec = tile("rec", [P, HALVES, KH, PACK], F32, "val_pl2")
-            for h in range(HALVES):
-                nc.vector.reciprocal(rec[:, h, :, :], den[h][:])
-            for h in range(HALVES):
-                for t in range(PACK):
-                    nc.scalar.activation(fac[h][:, :, t], rec[:, h, :, t], ACT.Copy, scale=os_col[:, t : t + 1])
+        value2_pool = tile("value2_pool", [P, T], BF16)
+        for c in range(2):
+            nc.scalar.copy(value2_pool[:, run_of(c, T // 2)], value2_part[c][:])
+        woven1 = tile("value_woven1", [P, P, PACK], BF16, "value2_part0")
+        turn_values("value_turned1", "v0", picked1, woven1[:])
+        picked2 = tile("picked_values2", [P, I], BF16)
+        nc.scalar.activation(picked2[:], value2_pool[:].indirect(token_list[:]), ACT.Copy)
+        picked3 = pick_values(3)
 
-        def weights(tag):
-            w_w = tile("w_w", [P, Q, PACK], BF16, tag)
-            for h in range(HALVES):
-                nc.vector.tensor_tensor(
-                    w_w[:, h * P : (h + 1) * P, :].rearrange("s (k j) t -> s k j t", j=GROUP),
-                    p_t[h][:].rearrange("s t (k j) -> s k j t", j=GROUP),
-                    fac[h][:].unsqueeze(2).to_broadcast([P, KH, GROUP, PACK]),
-                    ALU.mult,
-                )
-            return w_w
+        factor = tile("factor", [P, HALVES, GROUPS, PACK], F32, "value2_pool")
+        for h in range(HALVES):
+            for t in range(PACK):
+                nc.scalar.activation(factor[:, h, :, t], inverse[h][:, :, t], ACT.Copy, scale=os_col[:, t : t + 1])
 
-        val_g0 = gather_values(0)
-        mix0 = scores(0)
-        mix1 = scores(1)
-        exps(0, mix0)
-        exps(1, mix1)
-        val_wa = tile("val_wa", [P, 2 * P, PACK], BF16, "mix1")
-        turn_values(0, val_g0, val_wa)
-        turn_values(1, gather_values(1), val_wa)
-        nc.vector.tensor_copy(gain_g[:], gain_row[:].indirect(list_mem[:]))
-        group_sums()
-        val_wb = tile("val_wb", [P, 2 * P, PACK], BF16)
-        turn_values(2, gather_values(2), val_wb)
-        factors()
-        val_codes = tile("val_codes", [P, E], U32, "den0")
-        quantize_values(0, val_codes, val_wa)
-        turn_values(3, gather_values(3), val_wb)
+        woven23 = tile("value_woven23", [P, 2 * P, PACK], BF16)
+        turn_values("value_turned2", "v1", picked2, woven23[:, run_of(0, P), :])
+        turn_values("value_turned3", "v0", picked3, woven23[:, run_of(1, P), :])
+        value_codes = tile("value_codes", [P, E], U32, "denom0")
+        for t, woven in enumerate((woven0, woven1)):
+            quantize(value_codes, value_scales, run_of(t, P), woven[:])
+
         w_codes = tile("w_codes", [P, Q], U32)
         w_scales = tile("w_scales", [P, Q], U8)
         y = tile("y", [P, PACK, Q], F32)
-        y_w = [tile("y_w%d" % h, [P, P, PACK], BF16) for h in range(HALVES)]
+        y_woven = [tile("y_woven%d" % h, [P, P, PACK], BF16) for h in range(HALVES)]
         y_codes = tile("y_codes", [P, Q], U32)
         y_scales = tile("y_scales", [P, Q], U8)
-        back = []
+        o_back = [bank("o_back%d" % h, "a%d" % h, [P, PACK, P]) for h in range(HALVES)]
 
-        def product(h):
-            rows = slice(h * P, (h + 1) * P)
-            o_t = bank("o_t%d" % h, "b%d" % h, [P, E])
-            nc.tensor.matmul_mx(
-                out=o_t[:], lhsT=w_codes[:, rows].bitcast(FP8X4), lhsT_scale=w_scales[:, rows],
-                rhs=val_codes[:].bitcast(FP8X4), rhs_scale=val_scales[:], start=True, stop=True,
-            )
-            gained = tile("gained%d" % h, [P, PACK, P], F32)
-            nc.scalar.activation(
-                gained[:].rearrange("q t e -> q (t e)"), o_t[:], ACT.Copy, scale=gain_col[:, h : h + 1]
-            )
-            back.append(bank("back%d" % h, "a%d" % h, [P, PACK, P]))
-            for t in range(PACK):
-                nc.tensor.transpose(back[h][:, t, :], gained[:, t, :], ident[:])
-
-        def gather_members(tag=None):
-            mem_g = tile("mem_g", [P, PACK, Q], F32, tag)
-            for t in range(PACK):
-                nc.vector.tensor_copy(mem_g[:, t, :], mem_pl[t][:].indirect(list_mem[:]))
-            return mem_g
-
-        def finish(h, mem_g, copy):
-            rows = slice(h * P, (h + 1) * P)
-            nc.vector.tensor_tensor(y[:, :, rows], back[h][:], mem_g[:, :, rows], ALU.add)
-            nc.sync.dma_start(out_v[:, :, rows], y[:, :, rows])
-            weave(copy, y_w[h][:], y[:, :, rows])
-
-        w_w = weights("val_pl3")
+        w_woven = tile("w_woven", [P, Q, PACK], BF16, "value_plane3")
         for h in range(HALVES):
-            quantize_into(w_codes, w_scales, slice(h * P, (h + 1) * P), w_w[:, h * P : (h + 1) * P, :])
-        quantize_values(1, val_codes, val_wb)
-        gain_t = bank("gain_t", "p0", [P, HALVES, P])
+            nc.vector.tensor_tensor(
+                w_woven[:, run_of(h, P), :].rearrange("s (k j) t -> s k j t", j=GROUP),
+                p_turned[h][:].rearrange("s t (k j) -> s k j t", j=GROUP),
+                factor[:, h, :, :].unsqueeze(2).to_broadcast([P, GROUPS, GROUP, PACK]),
+                ALU.mult,
+            )
         for h in range(HALVES):
-            nc.tensor.transpose(gain_t[:, h, :], gain_g[:, h * P : (h + 1) * P], ident[:])
+            quantize(w_codes, w_scales, run_of(h, P), w_woven[:, run_of(h, P), :])
+        quantize(value_codes, value_scales, run_of(1, 2 * P), woven23[:])
+
+        gain_turned = bank("gain_turned", "p0", [P, HALVES, P])
+        for h in range(HALVES):
+            nc.tensor.transpose(gain_turned[:, h, :], picked_gain[:, run_of(h, P)], ident[:])
         gain_col = tile("gain_col", [P, HALVES], F32)
-        nc.scalar.copy(gain_col[:], gain_t[:, :, 0])
-        product(0)
-        product(1)
-        mem_g = gather_members("fac1")
-        finish(0, mem_g, SCOPY)
-        finish(1, mem_g, VCOPY)
+        nc.scalar.copy(gain_col[:], gain_turned[:, :, 0])
+
+        o_sum = {}
+        for u, tags in enumerate((("b0", "b1"), ("p1", "v1"))):
+            for h in range(HALVES):
+                rows, cols = run_of(h, P), run_of(u, 2 * P)
+                o_sum[h, u] = bank("o_sum%d%d" % (h, u), tags[h], [P, 2 * P])
+                nc.tensor.matmul_mx(
+                    out=o_sum[h, u][:], lhsT=w_codes[:, rows].bitcast(FP8X4), lhsT_scale=w_scales[:, rows],
+                    rhs=value_codes[:, cols].bitcast(FP8X4), rhs_scale=value_scales[:, cols], start=True, stop=True,
+                )
         for h in range(HALVES):
-            quantize_into(y_codes, y_scales, slice(h * P, (h + 1) * P), y_w[h][:])
-        nc.sync.dma_start(out_1[0].rearrange("p c r -> p (c r)").bitcast(I32), y_codes[:].bitcast(I32))
-        for quad in range(4):
+            for u in range(2):
+                gained = tile("gained%d%d" % (h, u), [P, 2, P], F32)
+                nc.scalar.activation(
+                    gained[:].rearrange("q x e -> q (x e)"), o_sum[h, u][:], ACT.Copy, scale=gain_col[:, h : h + 1]
+                )
+                for x in range(2):
+                    nc.tensor.transpose(o_back[h][:, 2 * u + x, :], gained[:, x, :], ident[:])
+
+        picked_members = tile("picked_members", [P, PACK, Q], F32, "value2_pool")
+        last = PACK - 1
+        for t in range(last):
+            gather(picked_members[:, t, :], member_plane[t][:], member_list[:])
+        for h in range(HALVES):
+            entries = member_list[:, run_of(h, P // PER_COLUMN)]
+            gather(picked_members[:, last, run_of(h, P)], member_plane[last][:], entries)
+
+        for h, copy in enumerate((nc.scalar.copy, nc.vector.tensor_copy)):
+            rows = run_of(h, P)
+            nc.vector.tensor_tensor(y[:, :, rows], o_back[h][:], picked_members[:, :, rows], ALU.add)
+            nc.sync.dma_start(out_v[:, :, rows], y[:, :, rows])
+            weave(copy, y_woven[h][:], y[:, :, rows])
+        for h in range(HALVES):
+            quantize(y_codes, y_scales, run_of(h, P), y_woven[h][:])
+        nc.scalar.dma_start(out_1[0].rearrange("p c r -> p (c r)").bitcast(I32), y_codes[:].bitcast(I32))
+        for quad in range(P // QUADRANT):
             queue = nc.scalar if quad % 2 else nc.sync
             queue.dma_start(
-                out_2[0, 4 * quad : 4 * quad + 4, :].bitcast(I32),
-                y_scales[32 * quad : 32 * quad + 4, :].bitcast(I32),
+                out_2[0, run_of(quad, PACK), :].bitcast(I32),
+                y_scales[QUADRANT * quad : QUADRANT * quad + PACK, :].bitcast(I32),
             )

@@ -67,7 +67,7 @@ def tile_attend_tilted_claimants_bymember_pl_kernel(
         key_words = tile("key_words", [P, T], U16)
         key_scales = tile("key_scales", [P, T], U8)
         gain_row = tile("gain_row", [P, M], F32)
-        note_planes = [tile("note_planes%d" % u, [P, 2, U], F32) for u in range(2)]
+        note_part = [[tile("note_part%d%d" % (u, c), [P, 2, U // 2], F32) for c in range(2)] for u in range(2)]
         value_plane = {t: tile("value_plane%d" % t, [P, T], F32) for t in (0, 1, 3)}
         value2_part = [tile("value2_part%d" % c, [P, T // 2], F32) for c in range(2)]
         member_plane = [tile("member_plane%d" % t, [P, M], F32) for t in range(PACK)]
@@ -84,6 +84,10 @@ def tile_attend_tilted_claimants_bymember_pl_kernel(
         member_v = member.rearrange("(p t) m -> p t m", t=PACK)
         out_v = out_0.rearrange("(p t) q -> p t q", t=PACK)
 
+        def load_notes(u):
+            for c in range(2):
+                nc.sync.dma_start(note_part[u][c][:], notes_v[:, run_of(u, 2), run_of(c, U // 2)])
+
         nc.gpsimd.memset(key_scales[:].bitcast(I32), 0)
         nc.vector.memset(lam_rows[:], 0.0)
         nc.vector.memset(gain_row[:], 0.0)
@@ -91,13 +95,13 @@ def tile_attend_tilted_claimants_bymember_pl_kernel(
 
         nc.sync.dma_start(token_list[:], offs)
         nc.sync.dma_start(key_words[:].bitcast(I32), keys_words[0].bitcast(I32))
-        nc.sync.dma_start(note_planes[0][:], notes_v[:, 0:2, :])
+        load_notes(0)
         for r in range(PACK):
             nc.sync.dma_start(
                 key_scales[r:P:QUADRANT, :].bitcast(I32), keys_scales[0, r:SCALE_ROWS:PACK, :].bitcast(I32)
             )
         nc.sync.dma_start(note_list[:], offs2)
-        nc.sync.dma_start(note_planes[1][:], notes_v[:, 2:4, :])
+        load_notes(1)
         nc.sync.dma_start(lam_rows[0:HALVES, :], lam.rearrange("(h p) o -> h (p o)", p=P))
         nc.sync.dma_start(q1_planes[:], query.rearrange("(p t) q -> p t q", t=PACK))
         nc.sync.dma_start(q2_planes[:], query2.rearrange("(p t) q -> p t q", t=PACK))
@@ -123,15 +127,12 @@ def tile_attend_tilted_claimants_bymember_pl_kernel(
         q1_codes, q2_codes = [tile(name, [P, Q], U32) for name in ("q1_codes", "q2_codes")]
         q1_scales, q2_scales = [tile(name, [P, Q], U8) for name in ("q1_scales", "q2_scales")]
 
-        def scalar_cast(out, in_):
-            nc.scalar.activation(out, in_, ACT.Copy)
-
         def pick_notes(u):
-            for c, copy in enumerate((scalar_cast, nc.vector.tensor_copy)):
-                cols = run_of(c, U // 2)
-                copy(
-                    note_pairs[u][:, cols].bitcast(BF16).rearrange("p (c x) -> p c x", x=2),
-                    note_planes[u][:, :, cols].rearrange("p x c -> p c x"),
+            for c in range(2):
+                nc.scalar.activation(
+                    note_pairs[u][:, run_of(c, U // 2)].bitcast(BF16).rearrange("p (c x) -> p c x", x=2),
+                    note_part[u][c][:].rearrange("p x c -> p c x"),
+                    ACT.Copy,
                 )
             halves = note_woven[:].rearrange("p i t -> p (i t)").bitcast(U32).rearrange("p (i u) -> p i u", u=2)
             gather(halves[:, :, u], note_pairs[u][:], note_list[:])
@@ -231,7 +232,7 @@ def tile_attend_tilted_claimants_bymember_pl_kernel(
         value2_pool = tile("value2_pool", [P, T], BF16)
         for c in range(2):
             nc.scalar.copy(value2_pool[:, run_of(c, T // 2)], value2_part[c][:])
-        woven1 = tile("value_woven1", [P, P, PACK], BF16, "value2_part0")
+        woven1 = tile("value_woven1", [P, P, PACK], BF16, "value2_part1")
         turn_values("value_turned1", "v0", picked1, woven1[:])
         picked2 = tile("picked_values2", [P, I], BF16)
         nc.scalar.activation(picked2[:], value2_pool[:].indirect(token_list[:]), ACT.Copy)
@@ -308,7 +309,7 @@ def tile_attend_tilted_claimants_bymember_pl_kernel(
             weave(copy, y_woven[h][:], y[:, :, rows])
         for h in range(HALVES):
             quantize(y_codes, y_scales, run_of(h, P), y_woven[h][:])
-        nc.scalar.dma_start(out_1[0].rearrange("p c r -> p (c r)").bitcast(I32), y_codes[:].bitcast(I32))
+        nc.sync.dma_start(out_1[0].rearrange("p c r -> p (c r)").bitcast(I32), y_codes[:].bitcast(I32))
         for quad in range(P // QUADRANT):
             queue = nc.scalar if quad % 2 else nc.sync
             queue.dma_start(

from contextlib import ExitStack

import concourse.mybir as mybir
from concourse.masks import make_identity

D, T, I, Q, E, U, M = 512, 2048, 512, 256, 512, 1024, 1024
P = 128
PACK = 4
GROUP = 8
HALVES = Q // P
GROUPS = P // GROUP
PER_COLUMN = 16
QUADRANT = 32
SCALE_ROWS = 16

FLOPS = 2 * D * Q * I * 2 + 2 * I * E * Q

F32 = mybir.dt.float32
BF16 = mybir.dt.bfloat16
I32 = mybir.dt.int32
U32 = mybir.dt.uint32
U16 = mybir.dt.uint16
U8 = mybir.dt.uint8
FP8X4 = mybir.dt.float8_e4m3fn_x4
FP4X4 = mybir.dt.float4_e2m1fn_x4
ALU = mybir.AluOpType
ACT = mybir.ActivationFunctionType
AX = mybir.AxisListType


def run_of(index, width):
    return slice(index * width, (index + 1) * width)


def tile_attend_tilted_claimants_bymember_pl_kernel(
    tc, query, query2, keys_words, keys_scales, notes, lam, sres, slot_factor, vals, member, mgain,
    offs, offs2, offs3, out_0, out_1, out_2,
):
    nc = tc.nc
    with ExitStack() as ctx:
        sb = ctx.enter_context(tc.tile_pool(name="sb", bufs=1))
        ps = ctx.enter_context(tc.psum_pool(name="ps", bufs=1))

        def tile(name, shape, dtype, tag=None):
            return sb.tile(shape, dtype, name=name, tag=tag or name, align_bytes=64)

        def bank(name, tag, shape):
            return ps.tile(shape, F32, name=name, tag=tag)

        def weave(copy, woven, planes):
            copy(
                woven.rearrange("p (c i) t -> p c t i", i=PACK),
                planes.rearrange("p t (c i) -> p c t i", i=PACK),
            )

        def quantize(codes, scales, cols, woven):
            nc.vector.quantize_mx(
                out=codes[:, cols].bitcast(FP8X4), scales=scales[:, cols], in_=woven.rearrange("p w t -> p (w t)")
            )

        def gather(out, window, entries):
            nc.vector.tensor_copy(out, window.indirect(entries))

        token_list = tile("token_list", [P, I // PER_COLUMN], U16)
        note_list = tile("note_list", [P, I // PER_COLUMN], U16)
        member_list = tile("member_list", [P, Q // PER_COLUMN], U16)
        key_words = tile("key_words", [P, T], U16)
        key_scales = tile("key_scales", [P, T], U8)
        gain_row = tile("gain_row", [P, M], F32)
        note_part = [[tile("note_part%d%d" % (u, c), [P, 2, U // 2], F32) for c in range(2)] for u in range(2)]
        value_plane = {t: tile("value_plane%d" % t, [P, T], F32) for t in (0, 1, 3)}
        value2_part = [tile("value2_part%d" % c, [P, T // 2], F32) for c in range(2)]
        member_plane = [tile("member_plane%d" % t, [P, M], F32) for t in range(PACK)]
        q1_planes = tile("q1_planes", [P, PACK, Q], F32)
        q2_planes = tile("q2_planes", [P, PACK, Q], F32)
        lam_col = tile("lam_col", [P, HALVES], F32)
        sres_col = tile("sres_col", [P, PACK], F32)
        os_col = tile("os_col", [P, PACK], F32)
        ident = tile("ident", [P, P], F32)
        lam_rows = tile("lam_rows", [P, P], F32)

        notes_v = notes.rearrange("(p t) u -> p t u", t=PACK)
        vals_v = vals.rearrange("(p t) n -> p t n", t=PACK)
        member_v = member.rearrange("(p t) m -> p t m", t=PACK)
        out_v = out_0.rearrange("(p t) q -> p t q", t=PACK)

        def load_notes(u):
            for c in range(2):
                nc.sync.dma_start(note_part[u][c][:], notes_v[:, run_of(u, 2), run_of(c, U // 2)])

        nc.gpsimd.memset(key_scales[:].bitcast(I32), 0)
        nc.vector.memset(lam_rows[:], 0.0)
        nc.vector.memset(gain_row[:], 0.0)
        make_identity(nc, ident[:])

        nc.sync.dma_start(token_list[:], offs)
        nc.sync.dma_start(key_words[:].bitcast(I32), keys_words[0].bitcast(I32))
        load_notes(0)
        for r in range(PACK):
            nc.sync.dma_start(
                key_scales[r:P:QUADRANT, :].bitcast(I32), keys_scales[0, r:SCALE_ROWS:PACK, :].bitcast(I32)
            )
        nc.sync.dma_start(note_list[:], offs2)
        load_notes(1)
        nc.sync.dma_start(lam_rows[0:HALVES, :], lam.rearrange("(h p) o -> h (p o)", p=P))
        nc.sync.dma_start(q1_planes[:], query.rearrange("(p t) q -> p t q", t=PACK))
        nc.sync.dma_start(q2_planes[:], query2.rearrange("(p t) q -> p t q", t=PACK))
        for t in range(2):
            nc.sync.dma_start(value_plane[t][:], vals_v[:, t, :])
        nc.sync.dma_start(member_list[:], offs3)
        nc.sync.dma_start(gain_row[0:1, :], mgain[0:1, :])
        nc.sync.dma_start(sres_col[:], sres.rearrange("(p t) o -> p (t o)", t=PACK))
        for c in range(2):
            nc.sync.dma_start(value2_part[c][:], vals_v[:, 2, run_of(c, T // 2)])
        nc.sync.dma_start(os_col[:], slot_factor.rearrange("o (p t) -> p (o t)", t=PACK))
        nc.sync.dma_start(value_plane[3][:], vals_v[:, 3, :])
        for t in range(PACK):
            nc.sync.dma_start(member_plane[t][:], member_v[:, t, :])

        picked_key_scales = tile("picked_key_scales", [P, I], U8)
        picked_key_words = tile("picked_key_words", [P, I], U16)
        note_pairs = [tile("note_pairs%d" % u, [P, U], U32) for u in range(2)]
        picked_gain = tile("picked_gain", [P, Q], F32)
        note_woven = tile("note_woven", [P, I, PACK], BF16)
        q1_woven = tile("q1_woven", [P, Q, PACK], BF16)
        q2_woven = tile("q2_woven", [P, Q, PACK], BF16)
        q1_codes, q2_codes = [tile(name, [P, Q], U32) for name in ("q1_codes", "q2_codes")]
        q1_scales, q2_scales = [tile(name, [P, Q], U8) for name in ("q1_scales", "q2_scales")]

        def pick_notes(u):
            for c in range(2):
                nc.scalar.activation(
                    note_pairs[u][:, run_of(c, U // 2)].bitcast(BF16).rearrange("p (c x) -> p c x", x=2),
                    note_part[u][c][:].rearrange("p x c -> p c x"),
                    ACT.Copy,
                )
            halves = note_woven[:].rearrange("p i t -> p (i t)").bitcast(U32).rearrange("p (i u) -> p i u", u=2)
            gather(halves[:, :, u], note_pairs[u][:], note_list[:])

        def quantize_queries(planes, woven, codes, scales):
            for h in range(HALVES):
                rows = run_of(h, P)
                weave(nc.scalar.copy, woven[:, rows, :], planes[:, :, rows])
                quantize(codes, scales, rows, woven[:, rows, :])

        gather(picked_key_words[:], key_words[:], token_list[:])
        gather(picked_key_scales[:], key_scales[:], token_list[:])
        for u in range(2):
            pick_notes(u)
        quantize_queries(q1_planes, q1_woven, q1_codes, q1_scales)
        note_codes = tile("note_codes", [P, I], U32, "q1_planes")
        note_scales = tile("note_scales", [P, I], U8)
        quantize(note_codes, note_scales, run_of(0, I), note_woven[:])
        quantize_queries(q2_planes, q2_woven, q2_codes, q2_scales)

        lam_turned = bank("lam_turned", "v1", [P, P])
        nc.tensor.transpose(lam_turned[:], lam_rows[:], ident[:])
        nc.vector.tensor_copy(lam_col[:], lam_turned[:, 0:HALVES])

        b_sum = [bank("b_sum%d" % h, "b%d" % h, [P, I]) for h in range(HALVES)]
        a_sum = [bank("a_sum%d" % h, "a%d" % h, [P, I]) for h in range(HALVES)]
        for h in range(HALVES):
            rows = run_of(h, P)
            nc.tensor.matmul_mx(
                out=a_sum[h][:], lhsT=q1_codes[:, rows].bitcast(FP8X4), lhsT_scale=q1_scales[:, rows],
                rhs=picked_key_words[:].bitcast(FP4X4), rhs_scale=picked_key_scales[:], start=True, stop=True,
            )
        gap = [tile("gap%d" % h, [P, I], F32) for h in range(HALVES)]
        for h in range(HALVES):
            nc.scalar.activation(gap[h][:], a_sum[h][:], ACT.Identity, scale=-1.0, bias=lam_col[:, h : h + 1])
        for h in range(HALVES):
            rows = run_of(h, P)
            nc.tensor.matmul_mx(
                out=b_sum[h][:], lhsT=q2_codes[:, rows].bitcast(FP8X4), lhsT_scale=q2_scales[:, rows],
                rhs=note_codes[:].bitcast(FP8X4), rhs_scale=note_scales[:], start=True, stop=True,
            )

        value_scales = tile("value_scales", [P, E], U8)

        def pick_values(t):
            picked = tile("picked_values%d" % t, [P, I], BF16)
            gather(picked[:], value_plane[t][:], token_list[:])
            return picked

        def turn_values(name, tag, picked, woven):
            pairs = picked[:].bitcast(F32)
            turned = bank(name, tag, [P, 2, P])
            for u in range(2):
                nc.tensor.transpose(turned[:, u, :], pairs[:, u : I // 2 : 2], ident[:])
            nc.scalar.copy(
                woven.rearrange("s e t -> s (e t)").bitcast(F32).rearrange("s (e u) -> s e u", u=2),
                turned[:].rearrange("s u e -> s e u"),
            )

        picked0 = pick_values(0)
        gated = []
        for h, tag in enumerate(("value_plane0", None)):
            tanh_b = tile("tanh_b%d" % h, [P, I], F32)
            nc.scalar.activation(tanh_b[:], b_sum[h][:], ACT.Tanh, scale=0.5)
            gated.append(tile("gated%d" % h, [P, I], F32, tag))
            nc.vector.scalar_tensor_tensor(gated[h][:], tanh_b[:], 1.0, gap[h][:], ALU.add, ALU.mult)
        p_turned = []
        for h in range(HALVES):
            p_dealt = tile("p_dealt%d" % h, [P, PACK, P], F32)
            nc.scalar.activation(
                p_dealt[:].rearrange("q t s -> q s t"), gated[h][:].rearrange("q (s t) -> q s t", t=PACK),
                ACT.Exp, scale=-0.5, bias=lam_col[:, h : h + 1],
            )
            p_turned.append(bank("p_turned%d" % h, "p%d" % h, [P, PACK, P]))
            for t in range(PACK):
                nc.tensor.transpose(p_turned[h][:, t, :], p_dealt[:, t, :], ident[:])

        woven0 = tile("value_woven0", [P, P, PACK], BF16, "gated1")
        turn_values("value_turned0", "v0", picked0, woven0[:])
        picked1 = pick_values(1)
        gather(picked_gain[:], gain_row[:], member_list[:])

        denom = [tile("denom%d" % h, [P, GROUPS, PACK], F32) for h in range(HALVES)]
        inverse = [tile("inverse%d" % h, [P, GROUPS, PACK], F32) for h in range(HALVES)]
        total = tile("total", [P, HALVES, GROUPS, PACK], F32, "value_plane1")
        for h in range(HALVES):
            nc.vector.tensor_reduce(
                total[:, h, :, :], p_turned[h][:].rearrange("s t (k j) -> s k t j", j=GROUP), AX.X, ALU.add
            )
        for h in range(HALVES):
            nc.vector.tensor_tensor(
                denom[h][:], total[:, h, :, :], sres_col[:].unsqueeze(1).to_broadcast([P, GROUPS, PACK]), ALU.add
            )
        for h in range(HALVES):
            nc.vector.reciprocal(inverse[h][:], denom[h][:])

        value2_pool = tile("value2_pool", [P, T], BF16)
        for c in range(2):
            nc.scalar.copy(value2_pool[:, run_of(c, T // 2)], value2_part[c][:])
        woven1 = tile("value_woven1", [P, P, PACK], BF16, "value2_part1")
        turn_values("value_turned1", "v0", picked1, woven1[:])
        picked2 = tile("picked_values2", [P, I], BF16)
        nc.scalar.activation(picked2[:], value2_pool[:].indirect(token_list[:]), ACT.Copy)
        picked3 = pick_values(3)

        factor = tile("factor", [P, HALVES, GROUPS, PACK], F32, "value2_pool")
        for h in range(HALVES):
            for t in range(PACK):
                nc.scalar.activation(factor[:, h, :, t], inverse[h][:, :, t], ACT.Copy, scale=os_col[:, t : t + 1])

        woven23 = tile("value_woven23", [P, 2 * P, PACK], BF16)
        turn_values("value_turned2", "v1", picked2, woven23[:, run_of(0, P), :])
        turn_values("value_turned3", "v0", picked3, woven23[:, run_of(1, P), :])
        value_codes = tile("value_codes", [P, E], U32, "denom0")
        for t, woven in enumerate((woven0, woven1)):
            quantize(value_codes, value_scales, run_of(t, P), woven[:])

        w_codes = tile("w_codes", [P, Q], U32)
        w_scales = tile("w_scales", [P, Q], U8)
        y = tile("y", [P, PACK, Q], F32)
        y_woven = [tile("y_woven%d" % h, [P, P, PACK], BF16) for h in range(HALVES)]
        y_codes = tile("y_codes", [P, Q], U32)
        y_scales = tile("y_scales", [P, Q], U8)
        o_back = [bank("o_back%d" % h, "a%d" % h, [P, PACK, P]) for h in range(HALVES)]

        w_woven = tile("w_woven", [P, Q, PACK], BF16, "value_plane3")
        for h in range(HALVES):
            nc.vector.tensor_tensor(
                w_woven[:, run_of(h, P), :].rearrange("s (k j) t -> s k j t", j=GROUP),
                p_turned[h][:].rearrange("s t (k j) -> s k j t", j=GROUP),
                factor[:, h, :, :].unsqueeze(2).to_broadcast([P, GROUPS, GROUP, PACK]),
                ALU.mult,
            )
        for h in range(HALVES):
            quantize(w_codes, w_scales, run_of(h, P), w_woven[:, run_of(h, P), :])
        quantize(value_codes, value_scales, run_of(1, 2 * P), woven23[:])

        gain_turned = bank("gain_turned", "p0", [P, HALVES, P])
        for h in range(HALVES):
            nc.tensor.transpose(gain_turned[:, h, :], picked_gain[:, run_of(h, P)], ident[:])
        gain_col = tile("gain_col", [P, HALVES], F32)
        nc.scalar.copy(gain_col[:], gain_turned[:, :, 0])

        o_sum = {}
        for u, tags in enumerate((("b0", "b1"), ("p1", "v1"))):
            for h in range(HALVES):
                rows, cols = run_of(h, P), run_of(u, 2 * P)
                o_sum[h, u] = bank("o_sum%d%d" % (h, u), tags[h], [P, 2 * P])
                nc.tensor.matmul_mx(
                    out=o_sum[h, u][:], lhsT=w_codes[:, rows].bitcast(FP8X4), lhsT_scale=w_scales[:, rows],
                    rhs=value_codes[:, cols].bitcast(FP8X4), rhs_scale=value_scales[:, cols], start=True, stop=True,
                )
        for h in range(HALVES):
            for u in range(2):
                gained = tile("gained%d%d" % (h, u), [P, 2, P], F32)
                nc.scalar.activation(
                    gained[:].rearrange("q x e -> q (x e)"), o_sum[h, u][:], ACT.Copy, scale=gain_col[:, h : h + 1]
                )
                for x in range(2):
                    nc.tensor.transpose(o_back[h][:, 2 * u + x, :], gained[:, x, :], ident[:])

        picked_members = tile("picked_members", [P, PACK, Q], F32, "value2_pool")
        last = PACK - 1
        for t in range(last):
            gather(picked_members[:, t, :], member_plane[t][:], member_list[:])
        for h in range(HALVES):
            entries = member_list[:, run_of(h, P // PER_COLUMN)]
            gather(picked_members[:, last, run_of(h, P)], member_plane[last][:], entries)

        for h, copy in enumerate((nc.scalar.copy, nc.vector.tensor_copy)):
            rows = run_of(h, P)
            nc.vector.tensor_tensor(y[:, :, rows], o_back[h][:], picked_members[:, :, rows], ALU.add)
            nc.sync.dma_start(out_v[:, :, rows], y[:, :, rows])
            weave(copy, y_woven[h][:], y[:, :, rows])
        for h in range(HALVES):
            quantize(y_codes, y_scales, run_of(h, P), y_woven[h][:])
        nc.sync.dma_start(out_1[0].rearrange("p c r -> p (c r)").bitcast(I32), y_codes[:].bitcast(I32))
        for quad in range(P // QUADRANT):
            queue = nc.scalar if quad % 2 else nc.sync
            queue.dma_start(
                out_2[0, run_of(quad, PACK), :].bitcast(I32),
                y_scales[QUADRANT * quad : QUADRANT * quad + PACK, :].bitcast(I32),
            )
